import numpy as np
import ml_dtypes


def mxq(x, axis, fmt="e4m3"):
    dtype, down = {"e4m3": (ml_dtypes.float8_e4m3fn, 7), "e5m2": (ml_dtypes.float8_e5m2, 14)}[fmt]
    v = np.moveaxis(np.asarray(x, np.float32).astype(ml_dtypes.bfloat16).astype(np.float64), axis, -1)
    blocks = v.reshape(v.shape[:-1] + (-1, 32))
    amax = np.abs(blocks).max(-1, keepdims=True)
    byte = np.maximum(np.where(amax > 0, np.frexp(amax)[1] - 1 + 127, 0) - down, 1)
    scale = np.exp2(byte - 127.0)
    codes = (blocks / scale).astype(np.float32).astype(dtype).astype(np.float64)
    return np.moveaxis((codes * scale).reshape(v.shape), -1, axis)


WIDE = False


def mx_kscale(k):
    if not WIDE:
        return np.ones(k)
    levels = np.array([10, -10, 5, -5, 0])
    if k % 512:
        return np.exp2(np.random.permutation(np.resize(levels, k // 32))).repeat(32)
    a = np.empty((k // 512, 16))
    for p in range(k // 512):
        a[p, :8] = np.random.permutation(np.resize(levels, 8))
        for g in range(8):
            far = levels[np.abs(levels - a[p, g]) >= 10]
            a[p, g + 8] = far[np.random.randint(len(far))]
    return np.exp2(a.ravel()).repeat(32)


def f64(x):
    return np.asarray(x).astype(np.float64)


def striped(idx):
    return np.tile(idx.reshape(-1, 16).T, (8, 1)).astype(np.uint16)


def unstriped(offs):
    return offs[:16].T.reshape(-1).astype(np.int64)


E2M1 = np.array([0.0, 0.5, 1.0, 1.5, 2.0, 3.0, 4.0, 6.0, -0.0, -0.5, -1.0, -1.5, -2.0, -3.0, -4.0, -6.0])


def pack_weight(w, fmt):
    k, n = w.shape
    w = f64(np.asarray(w, np.float32).astype(ml_dtypes.bfloat16)).reshape(k // 32, 32, n)
    amax = np.abs(w).max(1)
    if fmt == "e4m3":
        byte = np.frexp(amax)[1] - 1 + 127 - 7
    else:
        mant, ex = np.frexp(amax / 6.0)
        byte = np.where(mant > 0.5, ex, ex - 1) + 127
    byte = np.clip(np.where(amax > 0, byte, 1), 1, 254)
    scaled = (w * np.exp2(127.0 - byte)[:, None, :]).reshape(k, n).astype(np.float32)
    by_word = np.ascontiguousarray(scaled.reshape(k // 512, 128, 4, n).transpose(0, 1, 3, 2))
    if fmt == "e4m3":
        words = by_word.astype(ml_dtypes.float8_e4m3fn).view(np.uint8)
    else:
        c = by_word.astype(ml_dtypes.float4_e2m1fn).view(np.uint8) & 0xF
        words = (c[..., 0::2] | (c[..., 1::2] << 4)).reshape(k // 512, 128, 2 * n)
    return np.ascontiguousarray(words), np.ascontiguousarray(byte.astype(np.uint8).reshape(k // 512, 16, n))


def unpack_weight(words, scales, fmt):
    g, _, n = scales.shape
    words = np.ascontiguousarray(words).reshape(g, 128, n, -1)
    if fmt == "e4m3":
        vals = words.view(ml_dtypes.float8_e4m3fn).astype(np.float64)
    else:
        nib = np.empty((g, 128, n, 4), np.uint8)
        nib[..., 0::2] = words & 0xF
        nib[..., 1::2] = words >> 4
        vals = E2M1[nib]
    vals = vals * np.repeat(np.exp2(scales.astype(np.float64) - 127.0), 8, axis=1)[..., None]
    return vals.transpose(0, 1, 3, 2).reshape(g * 512, n)


def gelu(v):
    return 0.5 * v * (1.0 + np.tanh(np.sqrt(2.0 / np.pi) * (v + 0.044715 * v**3)))


K, K2, H, N, T, S = 512, 512, 1024, 256, 4096, 1024

def setup_inputs():
    n = np.random.standard_normal
    s = mx_kscale(K)[:, None]
    s2 = mx_kscale(K2)[:, None]
    u = mx_kscale(H)[:, None]
    d = {}
    d["tab_words"], d["tab_scales"] = pack_weight(n((K, T)) * s, "e4m3")
    d["offs"] = striped(np.random.permutation(T)[:S])
    d["xs_words"], d["xs_scales"] = pack_weight(n((K2, S)) * s2, "e4m3")
    d["w1"] = (n((K, H)) / K ** 0.5 / s * u.T).astype(np.float32)
    d["wx_words"], d["wx_scales"] = pack_weight(0.8 * n((K2, H)) / K2 ** 0.5 / s2 * u.T, "e2m1")
    d["rate"] = (np.exp(0.3 * n(H)) / u[:, 0]).astype(np.float32)
    d["span"] = np.random.uniform(1.2, 2.6, H).astype(np.float32)
    d["amp"] = (np.exp(0.3 * n(H)) * u[:, 0]).astype(np.float32)
    d["w3"] = (n((H, H)) / H ** 0.5 / u * u.T).astype(np.float32)
    d["w4_words"], d["w4_scales"] = pack_weight(n((H, N)) / H ** 0.5 / u, "e4m3")
    return d

def reference(tab_words, tab_scales, offs, xs_words, xs_scales, w1, wx_words, wx_scales,
              rate, span, amp, w3, w4_words, w4_scales):
    v = unpack_weight(tab_words, tab_scales, "e4m3")[:, unstriped(offs)]
    xs = unpack_weight(xs_words, xs_scales, "e4m3")
    wx = unpack_weight(wx_words, wx_scales, "e2m1")
    w4 = unpack_weight(w4_words, w4_scales, "e4m3")
    a = mxq(f64(w1), 0, "e4m3").T @ v
    b = wx.T @ xs
    phase = f64(span)[:, None] * np.tanh(f64(rate)[:, None] * a)
    h = f64(amp)[:, None] * np.sin(phase) - b
    c = mxq(f64(w3), 0, "e4m3").T @ mxq(h, 0, "e4m3")
    big = np.maximum(c, a)
    return w4.T @ mxq(big, 0, "e4m3")

@@ -1,0 +1,271 @@
+from contextlib import ExitStack
+
+import concourse.mybir as mybir
+
+K, H, N, T, S = 512, 1024, 256, 4096, 1024
+FLOPS = 2 * S * (K * H + K * H + H * H + H * N)
+
+F32 = mybir.dt.float32
+BF16 = mybir.dt.bfloat16
+I32 = mybir.dt.int32
+U32 = mybir.dt.uint32
+U16 = mybir.dt.uint16
+U8 = mybir.dt.uint8
+FP8X4 = mybir.dt.float8_e4m3fn_x4
+FP4X4 = mybir.dt.float4_e2m1fn_x4
+ACT = mybir.ActivationFunctionType
+ALU = mybir.AluOpType
+
+P = 128
+PACK = 4
+PASS = P * PACK
+GROUPS = H // PASS
+BANK = 512
+GATHER = 512
+TAB_ROW = 4
+CHUNKS = (512, 256, 256)
+
+
+def tile_list_drillship_thruster_features_kernel(
+    tc, tab_words, tab_scales, offs, xs_words, xs_scales, w1, wx_words, wx_scales,
+    rate, span, amp, w3, w4_words, w4_scales, out,
+):
+    nc = tc.nc
+    with ExitStack() as ctx:
+        keep = ctx.enter_context(tc.tile_pool(name="keep", bufs=1))
+        ring = ctx.enter_context(tc.tile_pool(name="ring", bufs=2))
+        psum = ctx.enter_context(tc.psum_pool(name="psum", bufs=1))
+
+        def held(name, shape, dtype):
+            return keep.tile(shape, dtype, name=name, align_bytes=64)
+
+        def staged(name, shape, dtype):
+            return ring.tile(shape, dtype, name=name, tag="staged", bufs=2, align_bytes=64)
+
+        def shared(tag):
+            return lambda name, shape, dtype: keep.tile(shape, dtype, name=name, tag=tag, align_bytes=64)
+
+        def cleared_plane(place, name, shape, engine):
+            plane = place(name, shape, U8)
+            engine.memset(plane[:].bitcast(I32), 0)
+            return plane
+
+        def load_scale_rows(queue, plane, rows, first):
+            for q in range(4):
+                queue.dma_start(
+                    out=plane[32 * q + first : 32 * q + first + 4].bitcast(I32),
+                    in_=rows[4 * q : 4 * q + 4].bitcast(I32),
+                )
+
+        def load_weight_rows(raw, w, g, mg):
+            rows = w[g * PASS : (g + 1) * PASS, mg * PASS : (mg + 1) * PASS]
+            nc.sync.dma_start(out=raw, in_=rows.rearrange("(p j) c -> p j c", j=PACK))
+            return raw
+
+        offsets = keep.tile([P, S // 16], U16, name="offsets")
+        nc.sync.dma_start(offsets[:], offs)
+        wx_raw = []
+        for g in range(GROUPS):
+            wx_raw.append(staged("wx_raw%d" % g, [P, 2 * PASS], U8))
+            nc.sync.dma_start(
+                out=wx_raw[g][:].bitcast(I32), in_=wx_words[0][:, 2 * PASS * g : 2 * PASS * (g + 1)].bitcast(I32)
+            )
+
+        wx_plane_raw = cleared_plane(held, "wx_plane_raw", [P, H], nc.vector)
+        tab_plane = cleared_plane(held, "tab_plane", [P, T], nc.vector)
+        zero_in = held("zero_in", [P, 1], F32)
+        nc.vector.memset(zero_in[:], 0.0)
+        zero = held("zero", [P, 1], F32)
+        nc.scalar.activation(zero[:], zero_in[:], ACT.Silu)
+        xs_plane = cleared_plane(held, "xs_plane", [P, S], nc.vector)
+
+        tab = shared("tab_bytes")("tab", [P, T], I32)
+        nc.sync.dma_start(out=tab[:], in_=tab_words[0].rearrange("p t i -> p (t i)").bitcast(I32))
+        load_scale_rows(nc.gpsimd, wx_plane_raw, wx_scales[0], 0)
+
+        channel = {}
+        for name, vec in (("rate", rate), ("span", span), ("amp", amp)):
+            channel[name] = held(name, [P, GROUPS, PACK], F32)
+            nc.scalar.dma_start(out=channel[name][:], in_=vec.rearrange("(g p t) -> p g t", g=GROUPS, t=PACK))
+
+        load_scale_rows(nc.scalar, tab_plane, tab_scales[0], TAB_ROW)
+        w1_raw = [load_weight_rows(staged("w1_raw%d" % g, [P, PACK, PASS], F32)[:], w1, 0, g) for g in range(GROUPS)]
+        load_scale_rows(nc.gpsimd, xs_plane, xs_scales[0], 0)
+        wx = held("wx", [P, 2 * H], U8)
+        for g in range(GROUPS):
+            nc.vector.tensor_copy(
+                out=wx[:, 2 * PASS * g : 2 * PASS * (g + 1)].rearrange("p (t m b) -> p m t b", t=PACK, b=2),
+                in_=wx_raw[g][:].rearrange("p (m t b) -> p m t b", t=PACK, b=2),
+            )
+
+        picked = {}
+
+        def gather(part):
+            piece = offsets[:, part * GATHER // 16 : (part + 1) * GATHER // 16]
+            words = held("v_words%d" % part, [P, GATHER], I32)
+            nc.vector.tensor_copy(out=words[:].bitcast(U32), in_=tab[:].bitcast(U32).indirect(piece))
+            plane = held("v_plane%d" % part, [P, GATHER], U8)
+            nc.vector.tensor_copy(out=plane[:], in_=tab_plane[:].indirect(piece))
+            picked[part] = (words, plane)
+
+        stationary = {}
+
+        def rotating(name, shape, dtype):
+            return ring.tile(shape, dtype, name=name, bufs=4, align_bytes=64)
+
+        def quantize_weight_pair(key, raw, u, copy, place=rotating):
+            grouped = place("w_grouped", [P, 2, P, PACK], BF16)
+            copy(
+                out=grouped[:].rearrange("p t m j -> p m j t"),
+                in_=raw.rearrange("p j (m u t) -> p u m j t", u=2, t=2)[:, u, :, :, :],
+            )
+            label = "%s%d%d%d" % (key + (u,))
+            codes = held("wq_" + label, [P, 2 * P], U32)
+            plane = held("ws_" + label, [P, 2 * P], U8)
+            nc.vector.quantize_mx(
+                out=codes[:].bitcast(FP8X4), scales=plane[:], in_=grouped[:].rearrange("p t m j -> p (t m j)")
+            )
+            for e in range(2):
+                stationary[key + (2 * u + e,)] = (codes[:, e * P : (e + 1) * P].bitcast(FP8X4), plane[:, e * P : (e + 1) * P])
+
+        def quantize(name, values, width):
+            codes = held(name + "_codes", [P, width], U32)
+            plane = held(name + "_plane", [P, width], U8)
+            nc.vector.quantize_mx(out=codes[:].bitcast(FP8X4), scales=plane[:], in_=values[:].rearrange("p n t -> p (n t)"))
+            return codes, plane
+
+        a_kept, h_mx, big_mx = {}, {}, {}
+
+        def first_stage(c, g, copy_a):
+            width, start = CHUNKS[c], sum(CHUNKS[:c])
+            per_bank = min(BANK // width, PACK)
+            words, plane = picked[start // GATHER]
+            here = slice(start % GATHER, start % GATHER + width)
+            cols = slice(start, start + width)
+            a_sb = held("a%d%d" % (c, g), [P, PACK, width], F32)
+            h_flat = ring.tile([P, PACK, width], BF16, name="h_flat", align_bytes=64)
+            for t0 in range(0, PACK, per_bank):
+                a_ps = psum.tile([P, per_bank, width], F32, name="a_ps", bufs=4)
+                b_ps = psum.tile([P, per_bank, width], F32, name="b_ps", bufs=2)
+                wave = ring.tile([P, per_bank, width], F32, name="wave", bufs=4)
+                bounded = ring.tile([P, per_bank, width], F32, name="bounded", bufs=3)
+                for e in range(per_bank):
+                    lhs, lhs_plane = stationary["w1", 0, g, t0 + e]
+                    nc.tensor.matmul_mx(
+                        out=a_ps[:, e, :], lhsT=lhs, lhsT_scale=lhs_plane,
+                        rhs=words[:, here].bitcast(FP8X4), rhs_scale=plane[TAB_ROW:P, here],
+                        start=True, stop=True,
+                    )
+                for e in range(per_bank):
+                    r = (g * PACK + t0 + e) * P
+                    nc.tensor.matmul_mx(
+                        out=b_ps[:, e, :], lhsT=wx[:, 2 * r : 2 * (r + P)].bitcast(FP4X4), lhsT_scale=wx_plane[:, r : r + P],
+                        rhs=xs[:, cols].bitcast(FP8X4), rhs_scale=xs_plane[:, cols],
+                        start=True, stop=True,
+                    )
+                for e in range(per_bank):
+                    t = t0 + e
+                    nc.scalar.activation(
+                        bounded[:, e, :], a_ps[:, e, :], ACT.Tanh, bias=zero[:], scale=channel["rate"][:, g, t : t + 1]
+                    )
+                copy_a(t0)(out=a_sb[:, t0 : t0 + per_bank, :], in_=a_ps[:])
+                for e in range(per_bank):
+                    t = t0 + e
+                    nc.scalar.activation(
+                        wave[:, e, :], bounded[:, e, :], ACT.Sin, bias=zero[:], scale=channel["span"][:, g, t : t + 1]
+                    )
+                for e in range(per_bank):
+                    t = t0 + e
+                    nc.vector.scalar_tensor_tensor(
+                        out=h_flat[:, t, :], in0=wave[:, e, :], scalar=channel["amp"][:, g, t : t + 1],
+                        in1=b_ps[:, e, :], op0=ALU.mult, op1=ALU.subtract,
+                    )
+            h = ring.tile([P, width, PACK], BF16, name="h", align_bytes=64)
+            nc.vector.tensor_copy(
+                out=h[:].rearrange("p (c i) t -> p c t i", i=4),
+                in_=h_flat[:].rearrange("p t (c i) -> p c t i", i=4),
+            )
+            a_kept[c, g] = a_sb
+            h_mx[c, g] = quantize("h%d%d" % (c, g), h, width)
+
+        def second_stage(c, mg):
+            width = CHUNKS[c]
+            big = ring.tile([P, width, PACK], BF16, name="big", align_bytes=64)
+            for n0 in range(0, width, P):
+                cols = slice(n0, n0 + P)
+                c_ps = psum.tile([P, PACK, P], F32, name="c_ps", bufs=2)
+                for t in range(PACK):
+                    for g in range(GROUPS):
+                        lhs, lhs_plane = stationary["w3", g, mg, t]
+                        codes, plane = h_mx[c, g]
+                        nc.tensor.matmul_mx(
+                            out=c_ps[:, t, :], lhsT=lhs, lhsT_scale=lhs_plane,
+                            rhs=codes[:, cols].bitcast(FP8X4), rhs_scale=plane[:, cols],
+                            start=(g == 0), stop=(g == GROUPS - 1),
+                        )
+                nc.vector.tensor_tensor(
+                    out=big[:, cols, :].rearrange("p (c i) t -> p c t i", i=2),
+                    in0=c_ps[:].rearrange("p t (c i) -> p c t i", i=2),
+                    in1=a_kept[c, mg][:, :, cols].rearrange("p t (c i) -> p c t i", i=2),
+                    op=ALU.max,
+                )
+            big_mx[c, mg] = quantize("big%d%d" % (c, mg), big, width)
+
+        def third_stage(c):
+            width, start = CHUNKS[c], sum(CHUNKS[:c])
+            for n0 in range(0, N, P):
+                o_ps = psum.tile([P, width], F32, name="a_ps", bufs=4)
+                for mg in range(GROUPS):
+                    codes, plane = big_mx[c, mg]
+                    nc.tensor.matmul_mx(
+                        out=o_ps[:], lhsT=w4[:, mg, n0 : n0 + P].bitcast(FP8X4), lhsT_scale=w4_plane[:, mg, n0 : n0 + P],
+                        rhs=codes[:].bitcast(FP8X4), rhs_scale=plane[:],
+                        start=(mg == 0), stop=(mg == GROUPS - 1),
+                    )
+                result = ring.tile([P, width], F32, name="result", bufs=4)
+                nc.scalar.copy(out=result[:], in_=o_ps[:])
+                nc.sync.dma_start(out=out[n0 : n0 + P, start : start + width], in_=result[:])
+
+        on_vector, on_scalar = nc.vector.tensor_copy, nc.scalar.copy
+
+        gather(0)
+        quantize_weight_pair(("w1", 0, 0), w1_raw[0], 0, on_vector, shared("xs_bytes"))
+        quantize_weight_pair(("w1", 0, 0), w1_raw[0], 1, on_scalar, shared("wx_plane_bytes"))
+        xs = shared("xs_bytes")("xs", [P, S], I32)
+        nc.sync.dma_start(out=xs[:], in_=xs_words[0].rearrange("p e i -> p (e i)").bitcast(I32))
+        wx_plane = shared("wx_plane_bytes")("wx_plane", [P, H], U8)
+        nc.vector.tensor_copy(
+            out=wx_plane[:].rearrange("p (g t m) -> p g m t", g=GROUPS, t=PACK),
+            in_=wx_plane_raw[:].rearrange("p (g m t) -> p g m t", g=GROUPS, t=PACK),
+        )
+
+        w3_raw = {}
+        for g in range(GROUPS):
+            w3_raw[g, 0] = load_weight_rows(staged("w3_raw%d" % g, [P, PACK, PASS], F32)[:], w3, g, 0)
+        w3_late = shared("tab_bytes")("w3_late", [P, GROUPS, PACK, PASS], F32)
+        for g in range(GROUPS):
+            w3_raw[g, 1] = load_weight_rows(w3_late[:, g, :, :], w3, g, 1)
+        w4 = staged("w4", [P, GROUPS, N], I32)
+        nc.sync.dma_start(out=w4[:], in_=w4_words.rearrange("a p e i -> p a (e i)").bitcast(I32))
+        w4_plane = cleared_plane(staged, "w4_plane", [P, GROUPS, N], nc.vector)
+        load_scale_rows(nc.sync, w4_plane, w4_scales.rearrange("a q e -> q a e"), 0)
+
+        first_stage(0, 0, lambda t0: on_scalar)
+        quantize_weight_pair(("w1", 0, 1), w1_raw[1], 0, on_vector)
+        quantize_weight_pair(("w1", 0, 1), w1_raw[1], 1, on_scalar)
+        gather(1)
+        first_stage(0, 1, lambda t0: on_scalar)
+        for g in range(GROUPS):
+            quantize_weight_pair(("w3", g, 0), w3_raw[g, 0], 0, on_scalar)
+            quantize_weight_pair(("w3", g, 0), w3_raw[g, 0], 1, on_vector)
+        for g in range(GROUPS):
+            quantize_weight_pair(("w3", g, 1), w3_raw[g, 1], 0, on_scalar)
+            quantize_weight_pair(("w3", g, 1), w3_raw[g, 1], 1, on_vector)
+        for c in range(1, len(CHUNKS)):
+            for g in range(GROUPS):
+                first_stage(c, g, lambda t0: on_scalar)
+                second_stage(c - 1, g)
+            third_stage(c - 1)
+        for mg in range(GROUPS):
+            second_stage(len(CHUNKS) - 1, mg)
+        third_stage(len(CHUNKS) - 1)

@@ -25,6 +25,17 @@ GATHER = 512
 TAB_ROW = 4
 CHUNKS = (512, 256, 256)
 
+RAW = PACK * PASS * 4
+AT_WX_PLANE_RAW = RAW
+AT_WX_RAW = RAW - 512
+AT_RAW = (0, RAW + H, 2 * RAW + H, 3 * RAW + H)
+AT_TAB = AT_RAW[2]
+AT_TAB_PLANE = AT_TAB + 4 * T
+AT_LATE_WORDS = AT_TAB_PLANE + T
+AT_WX_PLANE = AT_LATE_WORDS + 4 * GATHER
+AT_FIRST_PAIR = AT_WX_PLANE - 64
+AT_XS = AT_WX_PLANE + H
+
 
 def tile_list_drillship_thruster_features_kernel(
     tc, tab_words, tab_scales, offs, xs_words, xs_scales, w1, wx_words, wx_scales,
@@ -34,20 +45,18 @@ def tile_list_drillship_thruster_features_kernel(
     with ExitStack() as ctx:
         keep = ctx.enter_context(tc.tile_pool(name="keep", bufs=1))
         ring = ctx.enter_context(tc.tile_pool(name="ring", bufs=2))
+        arena = ctx.enter_context(tc.tile_pool(name="arena", bufs=1))
         psum = ctx.enter_context(tc.psum_pool(name="psum", bufs=1))
 
         def held(name, shape, dtype):
             return keep.tile(shape, dtype, name=name, align_bytes=64)
 
-        def staged(name, shape, dtype):
-            return ring.tile(shape, dtype, name=name, tag="staged", bufs=2, align_bytes=64)
+        def placed(offset):
+            return lambda name, shape, dtype: arena.tile(shape, dtype, name=name, offset=offset, align_bytes=64)
 
-        def shared(tag):
-            return lambda name, shape, dtype: keep.tile(shape, dtype, name=name, tag=tag, align_bytes=64)
-
-        def cleared_plane(place, name, shape, engine):
+        def cleared_plane(place, name, shape):
             plane = place(name, shape, U8)
-            engine.memset(plane[:].bitcast(I32), 0)
+            nc.vector.memset(plane[:].bitcast(I32), 0)
             return plane
 
         def load_scale_rows(queue, plane, rows, first):
@@ -64,61 +73,63 @@ def tile_list_drillship_thruster_features_kernel(
 
         offsets = keep.tile([P, S // 16], U16, name="offsets")
         nc.sync.dma_start(offsets[:], offs)
-        wx_raw = []
-        for g in range(GROUPS):
-            wx_raw.append(staged("wx_raw%d" % g, [P, 2 * PASS], U8))
-            nc.sync.dma_start(
-                out=wx_raw[g][:].bitcast(I32), in_=wx_words[0][:, 2 * PASS * g : 2 * PASS * (g + 1)].bitcast(I32)
-            )
+        wx_raw = placed(AT_WX_RAW)("wx_raw", [P, 2 * H], U8)
+        nc.sync.dma_start(out=wx_raw[:].bitcast(I32), in_=wx_words[0].bitcast(I32))
+        tab = placed(AT_TAB)("tab", [P, T], I32)
+        nc.sync.dma_start(out=tab[:], in_=tab_words[0].rearrange("p t i -> p (t i)").bitcast(I32))
 
-        wx_plane_raw = cleared_plane(held, "wx_plane_raw", [P, H], nc.vector)
-        tab_plane = cleared_plane(held, "tab_plane", [P, T], nc.vector)
+        tab_plane = cleared_plane(placed(AT_TAB_PLANE), "tab_plane", [P, T])
         zero_in = held("zero_in", [P, 1], F32)
         nc.vector.memset(zero_in[:], 0.0)
-        zero = held("zero", [P, 1], F32)
-        nc.scalar.activation(zero[:], zero_in[:], ACT.Silu)
-        xs_plane = cleared_plane(held, "xs_plane", [P, S], nc.vector)
-
-        tab = shared("tab_bytes")("tab", [P, T], I32)
-        nc.sync.dma_start(out=tab[:], in_=tab_words[0].rearrange("p t i -> p (t i)").bitcast(I32))
-        load_scale_rows(nc.gpsimd, wx_plane_raw, wx_scales[0], 0)
+        xs_plane = cleared_plane(held, "xs_plane", [P, S])
 
         channel = {}
-        for name, vec in (("rate", rate), ("span", span), ("amp", amp)):
+        for name, vec, queue in (("rate", rate, nc.scalar), ("span", span, nc.gpsimd), ("amp", amp, nc.gpsimd)):
             channel[name] = held(name, [P, GROUPS, PACK], F32)
-            nc.scalar.dma_start(out=channel[name][:], in_=vec.rearrange("(g p t) -> p g t", g=GROUPS, t=PACK))
-
+            queue.dma_start(out=channel[name][:], in_=vec.rearrange("(g p t) -> p g t", g=GROUPS, t=PACK))
         load_scale_rows(nc.scalar, tab_plane, tab_scales[0], TAB_ROW)
-        w1_raw = [load_weight_rows(staged("w1_raw%d" % g, [P, PACK, PASS], F32)[:], w1, 0, g) for g in range(GROUPS)]
         load_scale_rows(nc.gpsimd, xs_plane, xs_scales[0], 0)
+        zero = held("zero", [P, 1], F32)
+        nc.scalar.activation(zero[:], zero_in[:], ACT.Silu)
+
         wx = held("wx", [P, 2 * H], U8)
-        for g in range(GROUPS):
-            nc.vector.tensor_copy(
-                out=wx[:, 2 * PASS * g : 2 * PASS * (g + 1)].rearrange("p (t m b) -> p m t b", t=PACK, b=2),
-                in_=wx_raw[g][:].rearrange("p (m t b) -> p m t b", t=PACK, b=2),
-            )
+        nc.vector.tensor_copy(
+            out=wx[:].rearrange("p (g t m b) -> p g m t b", g=GROUPS, t=PACK, b=2),
+            in_=wx_raw[:].rearrange("p (g m t b) -> p g m t b", g=GROUPS, t=PACK, b=2),
+        )
+        w1_raw = [
+            load_weight_rows(placed(AT_RAW[g])("w1_raw%d" % g, [P, PACK, PASS], F32)[:], w1, 0, g) for g in range(GROUPS)
+        ]
 
-        picked = {}
+        wx_plane_raw = cleared_plane(placed(AT_WX_PLANE_RAW), "wx_plane_raw", [P, H])
+        load_scale_rows(nc.scalar, wx_plane_raw, wx_scales[0], 0)
 
-        def gather(part):
+        v_plane = held("v_plane", [P, S], U8)
+        nc.vector.tensor_copy(out=v_plane[:], in_=tab_plane[:].indirect(offsets[:]))
+        v_words = {}
+
+        def gather(part, place):
             piece = offsets[:, part * GATHER // 16 : (part + 1) * GATHER // 16]
-            words = held("v_words%d" % part, [P, GATHER], I32)
-            nc.vector.tensor_copy(out=words[:].bitcast(U32), in_=tab[:].bitcast(U32).indirect(piece))
-            plane = held("v_plane%d" % part, [P, GATHER], U8)
-            nc.vector.tensor_copy(out=plane[:], in_=tab_plane[:].indirect(piece))
-            picked[part] = (words, plane)
+            v_words[part] = place("v_words%d" % part, [P, GATHER], I32)
+            nc.vector.tensor_copy(out=v_words[part][:].bitcast(U32), in_=tab[:].bitcast(U32).indirect(piece))
 
         stationary = {}
 
         def rotating(name, shape, dtype):
-            return ring.tile(shape, dtype, name=name, bufs=4, align_bytes=64)
+            return ring.tile(shape, dtype, name=name, bufs=6, align_bytes=64)
 
-        def quantize_weight_pair(key, raw, u, copy, place=rotating):
+        rounded = {}
+
+        def round_weight_pair(key, raw, u, copy, place=rotating):
             grouped = place("w_grouped", [P, 2, P, PACK], BF16)
             copy(
                 out=grouped[:].rearrange("p t m j -> p m j t"),
                 in_=raw.rearrange("p j (m u t) -> p u m j t", u=2, t=2)[:, u, :, :, :],
             )
+            rounded[key, u] = grouped
+
+        def quantize_weight_pair(key, u):
+            grouped = rounded[key, u]
             label = "%s%d%d%d" % (key + (u,))
             codes = held("wq_" + label, [P, 2 * P], U32)
             plane = held("ws_" + label, [P, 2 * P], U8)
@@ -134,12 +145,12 @@ def tile_list_drillship_thruster_features_kernel(
             nc.vector.quantize_mx(out=codes[:].bitcast(FP8X4), scales=plane[:], in_=values[:].rearrange("p n t -> p (n t)"))
             return codes, plane
 
-        a_kept, h_mx, big_mx = {}, {}, {}
+        a_kept, h_rows, h_woven, h_mx, big, big_mx = {}, {}, {}, {}, {}, {}
 
-        def first_stage(c, g, copy_a):
+        def first_stage(c, g):
             width, start = CHUNKS[c], sum(CHUNKS[:c])
             per_bank = min(BANK // width, PACK)
-            words, plane = picked[start // GATHER]
+            words = v_words[start // GATHER]
             here = slice(start % GATHER, start % GATHER + width)
             cols = slice(start, start + width)
             a_sb = held("a%d%d" % (c, g), [P, PACK, width], F32)
@@ -153,7 +164,7 @@ def tile_list_drillship_thruster_features_kernel(
                     lhs, lhs_plane = stationary["w1", 0, g, t0 + e]
                     nc.tensor.matmul_mx(
                         out=a_ps[:, e, :], lhsT=lhs, lhsT_scale=lhs_plane,
-                        rhs=words[:, here].bitcast(FP8X4), rhs_scale=plane[TAB_ROW:P, here],
+                        rhs=words[:, here].bitcast(FP8X4), rhs_scale=v_plane[TAB_ROW:P, cols],
                         start=True, stop=True,
                     )
                 for e in range(per_bank):
@@ -168,7 +179,7 @@ def tile_list_drillship_thruster_features_kernel(
                     nc.scalar.activation(
                         bounded[:, e, :], a_ps[:, e, :], ACT.Tanh, bias=zero[:], scale=channel["rate"][:, g, t : t + 1]
                     )
-                copy_a(t0)(out=a_sb[:, t0 : t0 + per_bank, :], in_=a_ps[:])
+                nc.scalar.copy(out=a_sb[:, t0 : t0 + per_bank, :], in_=a_ps[:])
                 for e in range(per_bank):
                     t = t0 + e
                     nc.scalar.activation(
@@ -180,40 +191,45 @@ def tile_list_drillship_thruster_features_kernel(
                         out=h_flat[:, t, :], in0=wave[:, e, :], scalar=channel["amp"][:, g, t : t + 1],
                         in1=b_ps[:, e, :], op0=ALU.mult, op1=ALU.subtract,
                     )
-            h = ring.tile([P, width, PACK], BF16, name="h", align_bytes=64)
+            a_kept[c, g], h_rows[c, g] = a_sb, h_flat
+
+        def weave_h(c, g):
+            h_woven[c, g] = ring.tile([P, CHUNKS[c], PACK], BF16, name="h", align_bytes=64)
             nc.vector.tensor_copy(
-                out=h[:].rearrange("p (c i) t -> p c t i", i=4),
-                in_=h_flat[:].rearrange("p t (c i) -> p c t i", i=4),
+                out=h_woven[c, g][:].rearrange("p (c i) t -> p c t i", i=4),
+                in_=h_rows[c, g][:].rearrange("p t (c i) -> p c t i", i=4),
             )
-            a_kept[c, g] = a_sb
-            h_mx[c, g] = quantize("h%d%d" % (c, g), h, width)
 
-        def second_stage(c, mg):
-            width = CHUNKS[c]
-            big = ring.tile([P, width, PACK], BF16, name="big", align_bytes=64)
-            for n0 in range(0, width, P):
-                cols = slice(n0, n0 + P)
-                c_ps = psum.tile([P, PACK, P], F32, name="c_ps", bufs=2)
-                for t in range(PACK):
-                    for g in range(GROUPS):
-                        lhs, lhs_plane = stationary["w3", g, mg, t]
-                        codes, plane = h_mx[c, g]
-                        nc.tensor.matmul_mx(
-                            out=c_ps[:, t, :], lhsT=lhs, lhsT_scale=lhs_plane,
-                            rhs=codes[:, cols].bitcast(FP8X4), rhs_scale=plane[:, cols],
-                            start=(g == 0), stop=(g == GROUPS - 1),
-                        )
-                nc.vector.tensor_tensor(
-                    out=big[:, cols, :].rearrange("p (c i) t -> p c t i", i=2),
-                    in0=c_ps[:].rearrange("p t (c i) -> p c t i", i=2),
-                    in1=a_kept[c, mg][:, :, cols].rearrange("p t (c i) -> p c t i", i=2),
-                    op=ALU.max,
-                )
-            big_mx[c, mg] = quantize("big%d%d" % (c, mg), big, width)
+        def quantize_h(c, g):
+            h_mx[c, g] = quantize("h%d%d" % (c, g), h_woven[c, g], CHUNKS[c])
 
-        def third_stage(c):
+        def second_stage(c, mg, n0):
+            if n0 == 0:
+                big[c, mg] = ring.tile([P, CHUNKS[c], PACK], BF16, name="big", align_bytes=64)
+            cols = slice(n0, n0 + P)
+            c_ps = psum.tile([P, PACK, P], F32, name="c_ps", bufs=2)
+            for t in range(PACK):
+                for g in range(GROUPS):
+                    lhs, lhs_plane = stationary["w3", g, mg, t]
+                    codes, plane = h_mx[c, g]
+                    nc.tensor.matmul_mx(
+                        out=c_ps[:, t, :], lhsT=lhs, lhsT_scale=lhs_plane,
+                        rhs=codes[:, cols].bitcast(FP8X4), rhs_scale=plane[:, cols],
+                        start=(g == 0), stop=(g == GROUPS - 1),
+                    )
+            nc.vector.tensor_tensor(
+                out=big[c, mg][:, cols, :].rearrange("p (c i) t -> p c t i", i=2),
+                in0=c_ps[:].rearrange("p t (c i) -> p c t i", i=2),
+                in1=a_kept[c, mg][:, :, cols].rearrange("p t (c i) -> p c t i", i=2),
+                op=ALU.max,
+            )
+
+        def quantize_big(c, mg):
+            big_mx[c, mg] = quantize("big%d%d" % (c, mg), big[c, mg], CHUNKS[c])
+
+        def third_stage(c, copies):
             width, start = CHUNKS[c], sum(CHUNKS[:c])
-            for n0 in range(0, N, P):
+            for n0, copy in zip(range(0, N, P), copies):
                 o_ps = psum.tile([P, width], F32, name="a_ps", bufs=4)
                 for mg in range(GROUPS):
                     codes, plane = big_mx[c, mg]
@@ -223,49 +239,84 @@ def tile_list_drillship_thruster_features_kernel(
                         start=(mg == 0), stop=(mg == GROUPS - 1),
                     )
                 result = ring.tile([P, width], F32, name="result", bufs=4)
-                nc.scalar.copy(out=result[:], in_=o_ps[:])
+                copy(out=result[:], in_=o_ps[:])
                 nc.sync.dma_start(out=out[n0 : n0 + P, start : start + width], in_=result[:])
 
         on_vector, on_scalar = nc.vector.tensor_copy, nc.scalar.copy
 
-        gather(0)
-        quantize_weight_pair(("w1", 0, 0), w1_raw[0], 0, on_vector, shared("xs_bytes"))
-        quantize_weight_pair(("w1", 0, 0), w1_raw[0], 1, on_scalar, shared("wx_plane_bytes"))
-        xs = shared("xs_bytes")("xs", [P, S], I32)
+        gather(0, placed(AT_TAB_PLANE))
+        round_weight_pair(("w1", 0, 0), w1_raw[0], 0, on_vector, placed(AT_FIRST_PAIR))
+        round_weight_pair(("w1", 0, 0), w1_raw[0], 1, on_scalar)
+        for u in range(2):
+            quantize_weight_pair(("w1", 0, 0), u)
+        xs = placed(AT_XS)("xs", [P, S], I32)
         nc.sync.dma_start(out=xs[:], in_=xs_words[0].rearrange("p e i -> p (e i)").bitcast(I32))
-        wx_plane = shared("wx_plane_bytes")("wx_plane", [P, H], U8)
+        wx_plane = placed(AT_WX_PLANE)("wx_plane", [P, H], U8)
         nc.vector.tensor_copy(
             out=wx_plane[:].rearrange("p (g t m) -> p g m t", g=GROUPS, t=PACK),
             in_=wx_plane_raw[:].rearrange("p (g m t) -> p g m t", g=GROUPS, t=PACK),
         )
 
         w3_raw = {}
-        for g in range(GROUPS):
-            w3_raw[g, 0] = load_weight_rows(staged("w3_raw%d" % g, [P, PACK, PASS], F32)[:], w3, g, 0)
-        w3_late = shared("tab_bytes")("w3_late", [P, GROUPS, PACK, PASS], F32)
-        for g in range(GROUPS):
-            w3_raw[g, 1] = load_weight_rows(w3_late[:, g, :, :], w3, g, 1)
-        w4 = staged("w4", [P, GROUPS, N], I32)
+        for mg in range(GROUPS):
+            for g in range(GROUPS):
+                raw = placed(AT_RAW[GROUPS * mg + g])("w3_raw%d%d" % (g, mg), [P, PACK, PASS], F32)
+                w3_raw[g, mg] = load_weight_rows(raw[:], w3, g, mg)
+        w4 = placed(AT_RAW[0])("w4", [P, GROUPS, N], I32)
         nc.sync.dma_start(out=w4[:], in_=w4_words.rearrange("a p e i -> p a (e i)").bitcast(I32))
-        w4_plane = cleared_plane(staged, "w4_plane", [P, GROUPS, N], nc.vector)
+        w4_plane = cleared_plane(placed(AT_RAW[1]), "w4_plane", [P, GROUPS, N])
         load_scale_rows(nc.sync, w4_plane, w4_scales.rearrange("a q e -> q a e"), 0)
 
-        first_stage(0, 0, lambda t0: on_scalar)
-        quantize_weight_pair(("w1", 0, 1), w1_raw[1], 0, on_vector)
-        quantize_weight_pair(("w1", 0, 1), w1_raw[1], 1, on_scalar)
-        gather(1)
-        first_stage(0, 1, lambda t0: on_scalar)
+        first_stage(0, 0)
+        round_weight_pair(("w1", 0, 1), w1_raw[1], 0, on_vector)
+        round_weight_pair(("w1", 0, 1), w1_raw[1], 1, on_scalar)
+        gather(1, placed(AT_LATE_WORDS))
+        quantize_weight_pair(("w1", 0, 1), 0)
+        weave_h(0, 0)
+        quantize_weight_pair(("w1", 0, 1), 1)
         for g in range(GROUPS):
-            quantize_weight_pair(("w3", g, 0), w3_raw[g, 0], 0, on_scalar)
-            quantize_weight_pair(("w3", g, 0), w3_raw[g, 0], 1, on_vector)
+            for u in range(2):
+                round_weight_pair(("w3", g, 0), w3_raw[g, 0], u, on_vector)
+        quantize_h(0, 0)
+        first_stage(0, 1)
         for g in range(GROUPS):
-            quantize_weight_pair(("w3", g, 1), w3_raw[g, 1], 0, on_scalar)
-            quantize_weight_pair(("w3", g, 1), w3_raw[g, 1], 1, on_vector)
-        for c in range(1, len(CHUNKS)):
+            round_weight_pair(("w3", g, 1), w3_raw[g, 1], 1, on_scalar)
+        for u in range(2):
+            quantize_weight_pair(("w3", 0, 0), u)
+        weave_h(0, 1)
+        for u in range(2):
+            quantize_weight_pair(("w3", 1, 0), u)
+        quantize_h(0, 1)
+        for g in range(GROUPS):
+            round_weight_pair(("w3", g, 1), w3_raw[g, 1], 0, on_scalar)
+        for u in (1, 0):
             for g in range(GROUPS):
-                first_stage(c, g, lambda t0: on_scalar)
-                second_stage(c - 1, g)
-            third_stage(c - 1)
-        for mg in range(GROUPS):
-            second_stage(len(CHUNKS) - 1, mg)
-        third_stage(len(CHUNKS) - 1)
+                quantize_weight_pair(("w3", g, 1), u)
+
+        last = len(CHUNKS) - 1
+        for c in range(1, last + 1):
+            for g in range(GROUPS):
+                first_stage(c, g)
+                if g == 1:
+                    quantize_big(c - 1, 0)
+                elif c > 1:
+                    quantize_big(c - 2, 1)
+                    third_stage(c - 2, (on_scalar, on_scalar))
+                blocks = list(range(0, CHUNKS[c - 1], P))
+                second_stage(c - 1, g, blocks[0])
+                weave_h(c, g)
+                for n0 in blocks[1:2]:
+                    second_stage(c - 1, g, n0)
+                quantize_h(c, g)
+                for n0 in blocks[2:]:
+                    second_stage(c - 1, g, n0)
+        quantize_big(last - 1, 1)
+        third_stage(last - 1, (on_scalar, on_scalar))
+        for n0 in range(0, CHUNKS[last], P):
+            second_stage(last, 0, n0)
+        second_stage(last, 1, 0)
+        quantize_big(last, 0)
+        for n0 in range(P, CHUNKS[last], P):
+            second_stage(last, 1, n0)
+        quantize_big(last, 1)
+        third_stage(last, (on_scalar, on_vector))

@@ -26,15 +26,11 @@ TAB_ROW = 4
 CHUNKS = (512, 256, 256)
 
 RAW = PACK * PASS * 4
-AT_WX_PLANE_RAW = RAW
-AT_WX_RAW = RAW - 512
-AT_RAW = (0, RAW + H, 2 * RAW + H, 3 * RAW + H)
-AT_TAB = AT_RAW[2]
-AT_TAB_PLANE = AT_TAB + 4 * T
-AT_LATE_WORDS = AT_TAB_PLANE + T
-AT_WX_PLANE = AT_LATE_WORDS + 4 * GATHER
-AT_FIRST_PAIR = AT_WX_PLANE - 64
-AT_XS = AT_WX_PLANE + H
+AT_TAB = 2 * RAW
+AT_WX_PLANE_RAW = AT_TAB + 4 * T
+AT_WX_RAW = AT_WX_PLANE_RAW - 512
+AT_W1 = (0, RAW)
+AT_W3 = {(0, 0): 0, (1, 0): AT_TAB, (0, 1): AT_TAB + RAW, (1, 1): RAW}
 
 
 def tile_list_drillship_thruster_features_kernel(
@@ -75,10 +71,11 @@ def tile_list_drillship_thruster_features_kernel(
         nc.sync.dma_start(offsets[:], offs)
         wx_raw = placed(AT_WX_RAW)("wx_raw", [P, 2 * H], U8)
         nc.sync.dma_start(out=wx_raw[:].bitcast(I32), in_=wx_words[0].bitcast(I32))
-        tab = placed(AT_TAB)("tab", [P, T], I32)
-        nc.sync.dma_start(out=tab[:], in_=tab_words[0].rearrange("p t i -> p (t i)").bitcast(I32))
+        w1_raw = [load_weight_rows(placed(AT_W1[0])("w1_raw0", [P, PACK, PASS], F32)[:], w1, 0, 0)]
+        xs = held("xs", [P, S], I32)
+        nc.sync.dma_start(out=xs[:], in_=xs_words[0].rearrange("p e i -> p (e i)").bitcast(I32))
 
-        tab_plane = cleared_plane(placed(AT_TAB_PLANE), "tab_plane", [P, T])
+        tab_plane = cleared_plane(held, "tab_plane", [P, T])
         zero_in = held("zero_in", [P, 1], F32)
         nc.vector.memset(zero_in[:], 0.0)
         xs_plane = cleared_plane(held, "xs_plane", [P, S])
@@ -94,50 +91,46 @@ def tile_list_drillship_thruster_features_kernel(
 
         wx = held("wx", [P, 2 * H], U8)
         nc.vector.tensor_copy(
-            out=wx[:].rearrange("p (g t m b) -> p g m t b", g=GROUPS, t=PACK, b=2),
-            in_=wx_raw[:].rearrange("p (g m t b) -> p g m t b", g=GROUPS, t=PACK, b=2),
+            out=wx[:].bitcast(U16).rearrange("p (g t m) -> p g t m", g=GROUPS, t=PACK),
+            in_=wx_raw[:].bitcast(U16).rearrange("p (g m t) -> p g t m", g=GROUPS, t=PACK),
         )
-        w1_raw = [
-            load_weight_rows(placed(AT_RAW[g])("w1_raw%d" % g, [P, PACK, PASS], F32)[:], w1, 0, g) for g in range(GROUPS)
-        ]
-
+        tab = placed(AT_TAB)("tab", [P, T], I32)
+        nc.sync.dma_start(out=tab[:], in_=tab_words[0].rearrange("p t i -> p (t i)").bitcast(I32))
         wx_plane_raw = cleared_plane(placed(AT_WX_PLANE_RAW), "wx_plane_raw", [P, H])
         load_scale_rows(nc.scalar, wx_plane_raw, wx_scales[0], 0)
 
-        v_plane = held("v_plane", [P, S], U8)
-        nc.vector.tensor_copy(out=v_plane[:], in_=tab_plane[:].indirect(offsets[:]))
         v_words = {}
 
-        def gather(part, place):
+        def gather(part):
             piece = offsets[:, part * GATHER // 16 : (part + 1) * GATHER // 16]
-            v_words[part] = place("v_words%d" % part, [P, GATHER], I32)
+            v_words[part] = held("v_words%d" % part, [P, GATHER], I32)
             nc.vector.tensor_copy(out=v_words[part][:].bitcast(U32), in_=tab[:].bitcast(U32).indirect(piece))
 
         stationary = {}
 
-        def rotating(name, shape, dtype):
-            return ring.tile(shape, dtype, name=name, bufs=6, align_bytes=64)
-
         rounded = {}
 
-        def round_weight_pair(key, raw, u, copy, place=rotating):
-            grouped = place("w_grouped", [P, 2, P, PACK], BF16)
+        def rotating(name, shape, dtype):
+            return ring.tile(shape, dtype, name=name, bufs=4, align_bytes=64)
+
+        def round_weights(key, raw, u, copy, place=rotating):
+            if u == 0:
+                rounded[key] = place("w_rounded", [P, PACK, P, PACK], BF16)
             copy(
-                out=grouped[:].rearrange("p t m j -> p m j t"),
+                out=rounded[key][:, 2 * u : 2 * u + 2, :, :].rearrange("p t m j -> p m j t"),
                 in_=raw.rearrange("p j (m u t) -> p u m j t", u=2, t=2)[:, u, :, :, :],
             )
-            rounded[key, u] = grouped
 
-        def quantize_weight_pair(key, u):
-            grouped = rounded[key, u]
-            label = "%s%d%d%d" % (key + (u,))
-            codes = held("wq_" + label, [P, 2 * P], U32)
-            plane = held("ws_" + label, [P, 2 * P], U8)
+        def quantize_weights(key, t0, count):
+            label = "%s%d%d%d" % (key + (t0,))
+            codes = held("wq_" + label, [P, count * P], U32)
+            plane = held("ws_" + label, [P, count * P], U8)
             nc.vector.quantize_mx(
-                out=codes[:].bitcast(FP8X4), scales=plane[:], in_=grouped[:].rearrange("p t m j -> p (t m j)")
+                out=codes[:].bitcast(FP8X4), scales=plane[:],
+                in_=rounded[key][:, t0 : t0 + count, :, :].rearrange("p t m j -> p (t m j)"),
             )
-            for e in range(2):
-                stationary[key + (2 * u + e,)] = (codes[:, e * P : (e + 1) * P].bitcast(FP8X4), plane[:, e * P : (e + 1) * P])
+            for e in range(count):
+                stationary[key + (t0 + e,)] = (codes[:, e * P : (e + 1) * P].bitcast(FP8X4), plane[:, e * P : (e + 1) * P])
 
         def quantize(name, values, width):
             codes = held(name + "_codes", [P, width], U32)
@@ -156,7 +149,7 @@ def tile_list_drillship_thruster_features_kernel(
             a_sb = held("a%d%d" % (c, g), [P, PACK, width], F32)
             h_flat = ring.tile([P, PACK, width], BF16, name="h_flat", align_bytes=64)
             for t0 in range(0, PACK, per_bank):
-                a_ps = psum.tile([P, per_bank, width], F32, name="a_ps", bufs=4)
+                a_ps = psum.tile([P, per_bank, width], F32, name="a_ps", bufs=2)
                 b_ps = psum.tile([P, per_bank, width], F32, name="b_ps", bufs=2)
                 wave = ring.tile([P, per_bank, width], F32, name="wave", bufs=4)
                 bounded = ring.tile([P, per_bank, width], F32, name="bounded", bufs=3)
@@ -207,7 +200,7 @@ def tile_list_drillship_thruster_features_kernel(
             if n0 == 0:
                 big[c, mg] = ring.tile([P, CHUNKS[c], PACK], BF16, name="big", align_bytes=64)
             cols = slice(n0, n0 + P)
-            c_ps = psum.tile([P, PACK, P], F32, name="c_ps", bufs=2)
+            c_ps = psum.tile([P, PACK, P], F32, name="c_ps", bufs=4)
             for t in range(PACK):
                 for g in range(GROUPS):
                     lhs, lhs_plane = stationary["w3", g, mg, t]
@@ -230,7 +223,7 @@ def tile_list_drillship_thruster_features_kernel(
         def third_stage(c, copies):
             width, start = CHUNKS[c], sum(CHUNKS[:c])
             for n0, copy in zip(range(0, N, P), copies):
-                o_ps = psum.tile([P, width], F32, name="a_ps", bufs=4)
+                o_ps = psum.tile([P, width], F32, name="c_ps", bufs=4)
                 for mg in range(GROUPS):
                     codes, plane = big_mx[c, mg]
                     nc.tensor.matmul_mx(
@@ -244,54 +237,48 @@ def tile_list_drillship_thruster_features_kernel(
 
         on_vector, on_scalar = nc.vector.tensor_copy, nc.scalar.copy
 
-        gather(0, placed(AT_TAB_PLANE))
-        round_weight_pair(("w1", 0, 0), w1_raw[0], 0, on_vector, placed(AT_FIRST_PAIR))
-        round_weight_pair(("w1", 0, 0), w1_raw[0], 1, on_scalar)
-        for u in range(2):
-            quantize_weight_pair(("w1", 0, 0), u)
-        xs = placed(AT_XS)("xs", [P, S], I32)
-        nc.sync.dma_start(out=xs[:], in_=xs_words[0].rearrange("p e i -> p (e i)").bitcast(I32))
-        wx_plane = placed(AT_WX_PLANE)("wx_plane", [P, H], U8)
+        round_weights(("w1", 0, 0), w1_raw[0], 0, on_vector, placed(AT_W1[1]))
+        round_weights(("w1", 0, 0), w1_raw[0], 1, on_scalar)
+        quantize_weights(("w1", 0, 0), 0, PACK)
+        w1_raw.append(load_weight_rows(placed(AT_W1[1])("w1_raw1", [P, PACK, PASS], F32)[:], w1, 0, 1))
+        v_plane = held("v_plane", [P, S], U8)
+        nc.vector.tensor_copy(out=v_plane[:], in_=tab_plane[:].indirect(offsets[:]))
+        wx_plane = held("wx_plane", [P, H], U8)
         nc.vector.tensor_copy(
-            out=wx_plane[:].rearrange("p (g t m) -> p g m t", g=GROUPS, t=PACK),
-            in_=wx_plane_raw[:].rearrange("p (g m t) -> p g m t", g=GROUPS, t=PACK),
+            out=wx_plane[:].rearrange("p (g t m) -> p g t m", g=GROUPS, t=PACK),
+            in_=wx_plane_raw[:].rearrange("p (g m t) -> p g t m", g=GROUPS, t=PACK),
         )
-
+        for part in range(S // GATHER):
+            gather(part)
+        first_stage(0, 0)
+        round_weights(("w1", 0, 1), w1_raw[1], 0, on_vector)
+        round_weights(("w1", 0, 1), w1_raw[1], 1, on_scalar)
+        quantize_weights(("w1", 0, 1), 0, 2)
+        weave_h(0, 0)
+        quantize_weights(("w1", 0, 1), 2, 2)
         w3_raw = {}
         for mg in range(GROUPS):
             for g in range(GROUPS):
-                raw = placed(AT_RAW[GROUPS * mg + g])("w3_raw%d%d" % (g, mg), [P, PACK, PASS], F32)
+                raw = placed(AT_W3[g, mg])("w3_raw%d%d" % (g, mg), [P, PACK, PASS], F32)
                 w3_raw[g, mg] = load_weight_rows(raw[:], w3, g, mg)
-        w4 = placed(AT_RAW[0])("w4", [P, GROUPS, N], I32)
-        nc.sync.dma_start(out=w4[:], in_=w4_words.rearrange("a p e i -> p a (e i)").bitcast(I32))
-        w4_plane = cleared_plane(placed(AT_RAW[1]), "w4_plane", [P, GROUPS, N])
-        load_scale_rows(nc.sync, w4_plane, w4_scales.rearrange("a q e -> q a e"), 0)
-
-        first_stage(0, 0)
-        round_weight_pair(("w1", 0, 1), w1_raw[1], 0, on_vector)
-        round_weight_pair(("w1", 0, 1), w1_raw[1], 1, on_scalar)
-        gather(1, placed(AT_LATE_WORDS))
-        quantize_weight_pair(("w1", 0, 1), 0)
-        weave_h(0, 0)
-        quantize_weight_pair(("w1", 0, 1), 1)
         for g in range(GROUPS):
             for u in range(2):
-                round_weight_pair(("w3", g, 0), w3_raw[g, 0], u, on_vector)
+                round_weights(("w3", g, 0), w3_raw[g, 0], u, on_vector)
+        w4 = placed(0)("w4", [P, GROUPS, N], I32)
+        nc.sync.dma_start(out=w4[:], in_=w4_words.rearrange("a p e i -> p a (e i)").bitcast(I32))
+        w4_plane = cleared_plane(placed(4 * GROUPS * N), "w4_plane", [P, GROUPS, N])
+        load_scale_rows(nc.sync, w4_plane, w4_scales.rearrange("a q e -> q a e"), 0)
         quantize_h(0, 0)
         first_stage(0, 1)
-        for g in range(GROUPS):
-            round_weight_pair(("w3", g, 1), w3_raw[g, 1], 1, on_scalar)
-        for u in range(2):
-            quantize_weight_pair(("w3", 0, 0), u)
+        quantize_weights(("w3", 0, 0), 0, PACK)
         weave_h(0, 1)
-        for u in range(2):
-            quantize_weight_pair(("w3", 1, 0), u)
+        quantize_weights(("w3", 1, 0), 0, PACK)
         quantize_h(0, 1)
         for g in range(GROUPS):
-            round_weight_pair(("w3", g, 1), w3_raw[g, 1], 0, on_scalar)
-        for u in (1, 0):
-            for g in range(GROUPS):
-                quantize_weight_pair(("w3", g, 1), u)
+            for u in range(2):
+                round_weights(("w3", g, 1), w3_raw[g, 1], u, on_scalar)
+        for g in range(GROUPS):
+            quantize_weights(("w3", g, 1), 0, PACK)
 
         last = len(CHUNKS) - 1
         for c in range(1, last + 1):

@@ -29,8 +29,8 @@ RAW = PACK * PASS * 4
 AT_TAB = 2 * RAW
 AT_WX_PLANE_RAW = AT_TAB + 4 * T
 AT_WX_RAW = AT_WX_PLANE_RAW - 512
-AT_W1 = (0, RAW)
-AT_W3 = {(0, 0): 0, (1, 0): AT_TAB, (0, 1): AT_TAB + RAW, (1, 1): RAW}
+AT_XS = AT_WX_PLANE_RAW + H
+AT_W3 = {(0, 0): RAW, (1, 0): AT_TAB, (0, 1): AT_TAB + RAW, (1, 1): 0}
 
 
 def tile_list_drillship_thruster_features_kernel(
@@ -71,9 +71,7 @@ def tile_list_drillship_thruster_features_kernel(
         nc.sync.dma_start(offsets[:], offs)
         wx_raw = placed(AT_WX_RAW)("wx_raw", [P, 2 * H], U8)
         nc.sync.dma_start(out=wx_raw[:].bitcast(I32), in_=wx_words[0].bitcast(I32))
-        w1_raw = [load_weight_rows(placed(AT_W1[0])("w1_raw0", [P, PACK, PASS], F32)[:], w1, 0, 0)]
-        xs = held("xs", [P, S], I32)
-        nc.sync.dma_start(out=xs[:], in_=xs_words[0].rearrange("p e i -> p (e i)").bitcast(I32))
+        w1_raw = [load_weight_rows(placed(0)("w1_raw0", [P, PACK, PASS], F32)[:], w1, 0, 0)]
 
         tab_plane = cleared_plane(held, "tab_plane", [P, T])
         zero_in = held("zero_in", [P, 1], F32)
@@ -96,6 +94,8 @@ def tile_list_drillship_thruster_features_kernel(
         )
         tab = placed(AT_TAB)("tab", [P, T], I32)
         nc.sync.dma_start(out=tab[:], in_=tab_words[0].rearrange("p t i -> p (t i)").bitcast(I32))
+        xs = placed(AT_XS)("xs", [P, S], I32)
+        nc.sync.dma_start(out=xs[:], in_=xs_words[0].rearrange("p e i -> p (e i)").bitcast(I32))
         wx_plane_raw = cleared_plane(placed(AT_WX_PLANE_RAW), "wx_plane_raw", [P, H])
         load_scale_rows(nc.scalar, wx_plane_raw, wx_scales[0], 0)
 
@@ -237,10 +237,10 @@ def tile_list_drillship_thruster_features_kernel(
 
         on_vector, on_scalar = nc.vector.tensor_copy, nc.scalar.copy
 
-        round_weights(("w1", 0, 0), w1_raw[0], 0, on_vector, placed(AT_W1[1]))
-        round_weights(("w1", 0, 0), w1_raw[0], 1, on_scalar)
+        round_weights(("w1", 0, 0), w1_raw[0], 0, on_vector, placed(RAW))
+        round_weights(("w1", 0, 0), w1_raw[0], 1, on_vector)
         quantize_weights(("w1", 0, 0), 0, PACK)
-        w1_raw.append(load_weight_rows(placed(AT_W1[1])("w1_raw1", [P, PACK, PASS], F32)[:], w1, 0, 1))
+        w1_raw.append(load_weight_rows(placed(0)("w1_raw1", [P, PACK, PASS], F32)[:], w1, 0, 1))
         v_plane = held("v_plane", [P, S], U8)
         nc.vector.tensor_copy(out=v_plane[:], in_=tab_plane[:].indirect(offsets[:]))
         wx_plane = held("wx_plane", [P, H], U8)
@@ -264,9 +264,9 @@ def tile_list_drillship_thruster_features_kernel(
         for g in range(GROUPS):
             for u in range(2):
                 round_weights(("w3", g, 0), w3_raw[g, 0], u, on_vector)
-        w4 = placed(0)("w4", [P, GROUPS, N], I32)
+        w4 = placed(RAW)("w4", [P, GROUPS, N], I32)
         nc.sync.dma_start(out=w4[:], in_=w4_words.rearrange("a p e i -> p a (e i)").bitcast(I32))
-        w4_plane = cleared_plane(placed(4 * GROUPS * N), "w4_plane", [P, GROUPS, N])
+        w4_plane = cleared_plane(placed(RAW + 4 * GROUPS * N), "w4_plane", [P, GROUPS, N])
         load_scale_rows(nc.sync, w4_plane, w4_scales.rearrange("a q e -> q a e"), 0)
         quantize_h(0, 0)
         first_stage(0, 1)

from contextlib import ExitStack

import concourse.mybir as mybir

K, H, N, T, S = 512, 1024, 256, 4096, 1024
FLOPS = 2 * S * (K * H + K * H + H * H + H * N)

F32 = mybir.dt.float32
BF16 = mybir.dt.bfloat16
I32 = mybir.dt.int32
U32 = mybir.dt.uint32
U16 = mybir.dt.uint16
U8 = mybir.dt.uint8
FP8X4 = mybir.dt.float8_e4m3fn_x4
FP4X4 = mybir.dt.float4_e2m1fn_x4
ACT = mybir.ActivationFunctionType
ALU = mybir.AluOpType

P = 128
PACK = 4
PASS = P * PACK
GROUPS = H // PASS
BANK = 512
GATHER = 512
TAB_ROW = 4
CHUNKS = (512, 256, 256)

RAW = PACK * PASS * 4
AT_TAB = 2 * RAW
AT_WX_PLANE_RAW = AT_TAB + 4 * T
AT_WX_RAW = AT_WX_PLANE_RAW - 512
AT_XS = AT_WX_PLANE_RAW + H
AT_W3 = {(0, 0): RAW, (1, 0): AT_TAB, (0, 1): AT_TAB + RAW, (1, 1): 0}


def tile_list_drillship_thruster_features_kernel(
    tc, tab_words, tab_scales, offs, xs_words, xs_scales, w1, wx_words, wx_scales,
    rate, span, amp, w3, w4_words, w4_scales, out,
):
    nc = tc.nc
    with ExitStack() as ctx:
        keep = ctx.enter_context(tc.tile_pool(name="keep", bufs=1))
        ring = ctx.enter_context(tc.tile_pool(name="ring", bufs=2))
        arena = ctx.enter_context(tc.tile_pool(name="arena", bufs=1))
        psum = ctx.enter_context(tc.psum_pool(name="psum", bufs=1))

        def held(name, shape, dtype):
            return keep.tile(shape, dtype, name=name, align_bytes=64)

        def placed(offset):
            return lambda name, shape, dtype: arena.tile(shape, dtype, name=name, offset=offset, align_bytes=64)

        def cleared_plane(place, name, shape):
            plane = place(name, shape, U8)
            nc.vector.memset(plane[:].bitcast(I32), 0)
            return plane

        def load_scale_rows(queue, plane, rows, first):
            for q in range(4):
                queue.dma_start(
                    out=plane[32 * q + first : 32 * q + first + 4].bitcast(I32),
                    in_=rows[4 * q : 4 * q + 4].bitcast(I32),
                )

        def load_weight_rows(raw, w, g, mg):
            rows = w[g * PASS : (g + 1) * PASS, mg * PASS : (mg + 1) * PASS]
            nc.sync.dma_start(out=raw, in_=rows.rearrange("(p j) c -> p j c", j=PACK))
            return raw

        offsets = keep.tile([P, S // 16], U16, name="offsets")
        nc.sync.dma_start(offsets[:], offs)
        wx_raw = placed(AT_WX_RAW)("wx_raw", [P, 2 * H], U8)
        nc.sync.dma_start(out=wx_raw[:].bitcast(I32), in_=wx_words[0].bitcast(I32))
        w1_raw = [load_weight_rows(placed(0)("w1_raw0", [P, PACK, PASS], F32)[:], w1, 0, 0)]

        tab_plane = cleared_plane(held, "tab_plane", [P, T])
        zero_in = held("zero_in", [P, 1], F32)
        nc.vector.memset(zero_in[:], 0.0)
        xs_plane = cleared_plane(held, "xs_plane", [P, S])

        channel = {}
        for name, vec, queue in (("rate", rate, nc.scalar), ("span", span, nc.gpsimd), ("amp", amp, nc.gpsimd)):
            channel[name] = held(name, [P, GROUPS, PACK], F32)
            queue.dma_start(out=channel[name][:], in_=vec.rearrange("(g p t) -> p g t", g=GROUPS, t=PACK))
        load_scale_rows(nc.scalar, tab_plane, tab_scales[0], TAB_ROW)
        load_scale_rows(nc.gpsimd, xs_plane, xs_scales[0], 0)
        zero = held("zero", [P, 1], F32)
        nc.scalar.activation(zero[:], zero_in[:], ACT.Silu)

        wx = held("wx", [P, 2 * H], U8)
        nc.vector.tensor_copy(
            out=wx[:].bitcast(U16).rearrange("p (g t m) -> p g t m", g=GROUPS, t=PACK),
            in_=wx_raw[:].bitcast(U16).rearrange("p (g m t) -> p g t m", g=GROUPS, t=PACK),
        )
        tab = placed(AT_TAB)("tab", [P, T], I32)
        nc.sync.dma_start(out=tab[:], in_=tab_words[0].rearrange("p t i -> p (t i)").bitcast(I32))
        xs = placed(AT_XS)("xs", [P, S], I32)
        nc.sync.dma_start(out=xs[:], in_=xs_words[0].rearrange("p e i -> p (e i)").bitcast(I32))
        wx_plane_raw = cleared_plane(placed(AT_WX_PLANE_RAW), "wx_plane_raw", [P, H])
        load_scale_rows(nc.scalar, wx_plane_raw, wx_scales[0], 0)

        v_words = {}

        def gather(part):
            piece = offsets[:, part * GATHER // 16 : (part + 1) * GATHER // 16]
            v_words[part] = held("v_words%d" % part, [P, GATHER], I32)
            nc.vector.tensor_copy(out=v_words[part][:].bitcast(U32), in_=tab[:].bitcast(U32).indirect(piece))

        stationary = {}

        rounded = {}

        def rotating(name, shape, dtype):
            return ring.tile(shape, dtype, name=name, bufs=4, align_bytes=64)

        def round_weights(key, raw, u, copy, place=rotating):
            if u == 0:
                rounded[key] = place("w_rounded", [P, PACK, P, PACK], BF16)
            copy(
                out=rounded[key][:, 2 * u : 2 * u + 2, :, :].rearrange("p t m j -> p m j t"),
                in_=raw.rearrange("p j (m u t) -> p u m j t", u=2, t=2)[:, u, :, :, :],
            )

        def quantize_weights(key, t0, count):
            label = "%s%d%d%d" % (key + (t0,))
            codes = held("wq_" + label, [P, count * P], U32)
            plane = held("ws_" + label, [P, count * P], U8)
            nc.vector.quantize_mx(
                out=codes[:].bitcast(FP8X4), scales=plane[:],
                in_=rounded[key][:, t0 : t0 + count, :, :].rearrange("p t m j -> p (t m j)"),
            )
            for e in range(count):
                stationary[key + (t0 + e,)] = (codes[:, e * P : (e + 1) * P].bitcast(FP8X4), plane[:, e * P : (e + 1) * P])

        def quantize(name, values, width):
            codes = held(name + "_codes", [P, width], U32)
            plane = held(name + "_plane", [P, width], U8)
            nc.vector.quantize_mx(out=codes[:].bitcast(FP8X4), scales=plane[:], in_=values[:].rearrange("p n t -> p (n t)"))
            return codes, plane

        a_kept, h_rows, h_woven, h_mx, big, big_mx = {}, {}, {}, {}, {}, {}

        def first_stage(c, g):
            width, start = CHUNKS[c], sum(CHUNKS[:c])
            per_bank = min(BANK // width, PACK)
            words = v_words[start // GATHER]
            here = slice(start % GATHER, start % GATHER + width)
            cols = slice(start, start + width)
            a_sb = held("a%d%d" % (c, g), [P, PACK, width], F32)
            h_flat = ring.tile([P, PACK, width], BF16, name="h_flat", align_bytes=64)
            for t0 in range(0, PACK, per_bank):
                a_ps = psum.tile([P, per_bank, width], F32, name="a_ps", bufs=2)
                b_ps = psum.tile([P, per_bank, width], F32, name="b_ps", bufs=2)
                wave = ring.tile([P, per_bank, width], F32, name="wave", bufs=4)
                bounded = ring.tile([P, per_bank, width], F32, name="bounded", bufs=3)
                for e in range(per_bank):
                    lhs, lhs_plane = stationary["w1", 0, g, t0 + e]
                    nc.tensor.matmul_mx(
                        out=a_ps[:, e, :], lhsT=lhs, lhsT_scale=lhs_plane,
                        rhs=words[:, here].bitcast(FP8X4), rhs_scale=v_plane[TAB_ROW:P, cols],
                        start=True, stop=True,
                    )
                for e in range(per_bank):
                    r = (g * PACK + t0 + e) * P
                    nc.tensor.matmul_mx(
                        out=b_ps[:, e, :], lhsT=wx[:, 2 * r : 2 * (r + P)].bitcast(FP4X4), lhsT_scale=wx_plane[:, r : r + P],
                        rhs=xs[:, cols].bitcast(FP8X4), rhs_scale=xs_plane[:, cols],
                        start=True, stop=True,
                    )
                for e in range(per_bank):
                    t = t0 + e
                    nc.scalar.activation(
                        bounded[:, e, :], a_ps[:, e, :], ACT.Tanh, bias=zero[:], scale=channel["rate"][:, g, t : t + 1]
                    )
                nc.scalar.copy(out=a_sb[:, t0 : t0 + per_bank, :], in_=a_ps[:])
                for e in range(per_bank):
                    t = t0 + e
                    nc.scalar.activation(
                        wave[:, e, :], bounded[:, e, :], ACT.Sin, bias=zero[:], scale=channel["span"][:, g, t : t + 1]
                    )
                for e in range(per_bank):
                    t = t0 + e
                    nc.vector.scalar_tensor_tensor(
                        out=h_flat[:, t, :], in0=wave[:, e, :], scalar=channel["amp"][:, g, t : t + 1],
                        in1=b_ps[:, e, :], op0=ALU.mult, op1=ALU.subtract,
                    )
            a_kept[c, g], h_rows[c, g] = a_sb, h_flat

        def weave_h(c, g):
            h_woven[c, g] = ring.tile([P, CHUNKS[c], PACK], BF16, name="h", align_bytes=64)
            nc.vector.tensor_copy(
                out=h_woven[c, g][:].rearrange("p (c i) t -> p c t i", i=4),
                in_=h_rows[c, g][:].rearrange("p t (c i) -> p c t i", i=4),
            )

        def quantize_h(c, g):
            h_mx[c, g] = quantize("h%d%d" % (c, g), h_woven[c, g], CHUNKS[c])

        def second_stage(c, mg, n0):
            if n0 == 0:
                big[c, mg] = ring.tile([P, CHUNKS[c], PACK], BF16, name="big", align_bytes=64)
            cols = slice(n0, n0 + P)
            c_ps = psum.tile([P, PACK, P], F32, name="c_ps", bufs=4)
            for t in range(PACK):
                for g in range(GROUPS):
                    lhs, lhs_plane = stationary["w3", g, mg, t]
                    codes, plane = h_mx[c, g]
                    nc.tensor.matmul_mx(
                        out=c_ps[:, t, :], lhsT=lhs, lhsT_scale=lhs_plane,
                        rhs=codes[:, cols].bitcast(FP8X4), rhs_scale=plane[:, cols],
                        start=(g == 0), stop=(g == GROUPS - 1),
                    )
            nc.vector.tensor_tensor(
                out=big[c, mg][:, cols, :].rearrange("p (c i) t -> p c t i", i=2),
                in0=c_ps[:].rearrange("p t (c i) -> p c t i", i=2),
                in1=a_kept[c, mg][:, :, cols].rearrange("p t (c i) -> p c t i", i=2),
                op=ALU.max,
            )

        def quantize_big(c, mg):
            big_mx[c, mg] = quantize("big%d%d" % (c, mg), big[c, mg], CHUNKS[c])

        def third_stage(c, copies):
            width, start = CHUNKS[c], sum(CHUNKS[:c])
            for n0, copy in zip(range(0, N, P), copies):
                o_ps = psum.tile([P, width], F32, name="c_ps", bufs=4)
                for mg in range(GROUPS):
                    codes, plane = big_mx[c, mg]
                    nc.tensor.matmul_mx(
                        out=o_ps[:], lhsT=w4[:, mg, n0 : n0 + P].bitcast(FP8X4), lhsT_scale=w4_plane[:, mg, n0 : n0 + P],
                        rhs=codes[:].bitcast(FP8X4), rhs_scale=plane[:],
                        start=(mg == 0), stop=(mg == GROUPS - 1),
                    )
                result = ring.tile([P, width], F32, name="result", bufs=4)
                copy(out=result[:], in_=o_ps[:])
                nc.sync.dma_start(out=out[n0 : n0 + P, start : start + width], in_=result[:])

        on_vector, on_scalar = nc.vector.tensor_copy, nc.scalar.copy

        round_weights(("w1", 0, 0), w1_raw[0], 0, on_vector, placed(RAW))
        round_weights(("w1", 0, 0), w1_raw[0], 1, on_vector)
        quantize_weights(("w1", 0, 0), 0, PACK)
        w1_raw.append(load_weight_rows(placed(0)("w1_raw1", [P, PACK, PASS], F32)[:], w1, 0, 1))
        v_plane = held("v_plane", [P, S], U8)
        nc.vector.tensor_copy(out=v_plane[:], in_=tab_plane[:].indirect(offsets[:]))
        wx_plane = held("wx_plane", [P, H], U8)
        nc.vector.tensor_copy(
            out=wx_plane[:].rearrange("p (g t m) -> p g t m", g=GROUPS, t=PACK),
            in_=wx_plane_raw[:].rearrange("p (g m t) -> p g t m", g=GROUPS, t=PACK),
        )
        for part in range(S // GATHER):
            gather(part)
        first_stage(0, 0)
        round_weights(("w1", 0, 1), w1_raw[1], 0, on_vector)
        round_weights(("w1", 0, 1), w1_raw[1], 1, on_scalar)
        quantize_weights(("w1", 0, 1), 0, 2)
        weave_h(0, 0)
        quantize_weights(("w1", 0, 1), 2, 2)
        w3_raw = {}
        for mg in range(GROUPS):
            for g in range(GROUPS):
                raw = placed(AT_W3[g, mg])("w3_raw%d%d" % (g, mg), [P, PACK, PASS], F32)
                w3_raw[g, mg] = load_weight_rows(raw[:], w3, g, mg)
        for g in range(GROUPS):
            for u in range(2):
                round_weights(("w3", g, 0), w3_raw[g, 0], u, on_vector)
        w4 = placed(RAW)("w4", [P, GROUPS, N], I32)
        nc.sync.dma_start(out=w4[:], in_=w4_words.rearrange("a p e i -> p a (e i)").bitcast(I32))
        w4_plane = cleared_plane(placed(RAW + 4 * GROUPS * N), "w4_plane", [P, GROUPS, N])
        load_scale_rows(nc.sync, w4_plane, w4_scales.rearrange("a q e -> q a e"), 0)
        quantize_h(0, 0)
        first_stage(0, 1)
        quantize_weights(("w3", 0, 0), 0, PACK)
        weave_h(0, 1)
        quantize_weights(("w3", 1, 0), 0, PACK)
        quantize_h(0, 1)
        for g in range(GROUPS):
            for u in range(2):
                round_weights(("w3", g, 1), w3_raw[g, 1], u, on_scalar)
        for g in range(GROUPS):
            quantize_weights(("w3", g, 1), 0, PACK)

        last = len(CHUNKS) - 1
        for c in range(1, last + 1):
            for g in range(GROUPS):
                first_stage(c, g)
                if g == 1:
                    quantize_big(c - 1, 0)
                elif c > 1:
                    quantize_big(c - 2, 1)
                    third_stage(c - 2, (on_scalar, on_scalar))
                blocks = list(range(0, CHUNKS[c - 1], P))
                second_stage(c - 1, g, blocks[0])
                weave_h(c, g)
                for n0 in blocks[1:2]:
                    second_stage(c - 1, g, n0)
                quantize_h(c, g)
                for n0 in blocks[2:]:
                    second_stage(c - 1, g, n0)
        quantize_big(last - 1, 1)
        third_stage(last - 1, (on_scalar, on_scalar))
        for n0 in range(0, CHUNKS[last], P):
            second_stage(last, 0, n0)
        second_stage(last, 1, 0)
        quantize_big(last, 0)
        for n0 in range(P, CHUNKS[last], P):
            second_stage(last, 1, n0)
        quantize_big(last, 1)
        third_stage(last, (on_scalar, on_vector))
